import numpy as np
import ml_dtypes


def mxq(x, axis, fmt="e4m3"):
    dtype, down = {"e4m3": (ml_dtypes.float8_e4m3fn, 7), "e5m2": (ml_dtypes.float8_e5m2, 14)}[fmt]
    v = np.moveaxis(np.asarray(x, np.float32).astype(ml_dtypes.bfloat16).astype(np.float64), axis, -1)
    blocks = v.reshape(v.shape[:-1] + (-1, 32))
    amax = np.abs(blocks).max(-1, keepdims=True)
    byte = np.maximum(np.where(amax > 0, np.frexp(amax)[1] - 1 + 127, 0) - down, 1)
    scale = np.exp2(byte - 127.0)
    codes = (blocks / scale).astype(np.float32).astype(dtype).astype(np.float64)
    return np.moveaxis((codes * scale).reshape(v.shape), -1, axis)


WIDE = False


def mx_kscale(k):
    if not WIDE:
        return np.ones(k)
    levels = np.array([10, -10, 5, -5, 0])
    if k % 512:
        return np.exp2(np.random.permutation(np.resize(levels, k // 32))).repeat(32)
    a = np.empty((k // 512, 16))
    for p in range(k // 512):
        a[p, :8] = np.random.permutation(np.resize(levels, 8))
        for g in range(8):
            far = levels[np.abs(levels - a[p, g]) >= 10]
            a[p, g + 8] = far[np.random.randint(len(far))]
    return np.exp2(a.ravel()).repeat(32)


def f64(x):
    return np.asarray(x).astype(np.float64)


def striped(idx):
    return np.tile(idx.reshape(-1, 16).T, (8, 1)).astype(np.uint16)


def unstriped(offs):
    return offs[:16].T.reshape(-1).astype(np.int64)


def striped8(idx):
    return np.concatenate([x.reshape(-1, 16).T for x in idx]).astype(np.uint16)


def runs(offs, k):
    lists = np.stack([offs[16 * r : 16 * r + 16].T.reshape(-1) for r in range(8)]).astype(np.int64)
    return lists[np.arange(k) % 512 // 64]


def pack_weight(w):
    k, n = w.shape
    w = f64(np.asarray(w, np.float32).astype(ml_dtypes.bfloat16)).reshape(k // 32, 32, n)
    amax = np.abs(w).max(1)
    byte = np.clip(np.where(amax > 0, np.frexp(amax)[1] - 1 + 127 - 7, 1), 1, 254)
    scaled = (w * np.exp2(127.0 - byte)[:, None, :]).reshape(k, n).astype(np.float32)
    words = np.ascontiguousarray(scaled.reshape(k // 512, 128, 4, n).transpose(0, 1, 3, 2)).astype(ml_dtypes.float8_e4m3fn).view(np.uint8)
    return words, np.ascontiguousarray(byte.astype(np.uint8).reshape(k // 512, 16, n))


def unpack_weight(words, scales):
    g, p, n, _ = words.shape
    vals = np.ascontiguousarray(words).view(ml_dtypes.float8_e4m3fn).astype(np.float64) * np.repeat(np.exp2(scales.astype(np.float64) - 127.0), 8, axis=1)[..., None]
    return vals.transpose(0, 1, 3, 2).reshape(g * 512, n)


E2M1 = np.array([0.0, 0.5, 1.0, 1.5, 2.0, 3.0, 4.0, 6.0, -0.0, -0.5, -1.0, -1.5, -2.0, -3.0, -4.0, -6.0])


def pack_fp4(w):
    k, n = w.shape
    w = f64(np.asarray(w, np.float32).astype(ml_dtypes.bfloat16)).reshape(k // 32, 32, n)
    amax = np.abs(w).max(1)
    mant, ex = np.frexp(amax / 6.0)
    byte = np.clip(np.where(amax > 0, np.where(mant > 0.5, ex, ex - 1) + 127, 1), 1, 254)
    scaled = (w * np.exp2(127.0 - byte)[:, None, :]).reshape(k, n).astype(np.float32)
    c = np.ascontiguousarray(scaled.reshape(k // 512, 128, 4, n).transpose(0, 1, 3, 2)).astype(ml_dtypes.float4_e2m1fn).view(np.uint8) & 0xF
    words = (c[..., 0::2] | (c[..., 1::2] << 4)).reshape(k // 512, 128, 2 * n)
    return np.ascontiguousarray(words), np.ascontiguousarray(byte.astype(np.uint8).reshape(k // 512, 16, n))


def unpack_fp4(words, scales):
    g, _, n = scales.shape
    words = np.ascontiguousarray(words).reshape(g, 128, n, 2)
    nib = np.empty((g, 128, n, 4), np.uint8)
    nib[..., 0::2] = words & 0xF
    nib[..., 1::2] = words >> 4
    vals = E2M1[nib] * np.repeat(np.exp2(scales.astype(np.float64) - 127.0), 8, axis=1)[..., None]
    return vals.transpose(0, 1, 3, 2).reshape(g * 512, n)


def planes(y):
    n, m = y.shape
    v = y.astype(np.float32).astype(ml_dtypes.bfloat16).astype(np.float64).reshape(n // 32, 32, m)
    top = np.abs(v).max(1)
    byte = np.clip(np.where(top > 0, np.frexp(top)[1] - 1 + 127 - 7, 1), 1, 254)
    codes = (v * np.exp2(127.0 - byte)[:, None, :]).reshape(n, m).astype(np.float32).astype(ml_dtypes.float8_e4m3fn).view(np.uint8)
    words = codes.reshape(n // 512, 128, 4, m).transpose(0, 1, 3, 2)
    return np.ascontiguousarray(words), np.ascontiguousarray(byte.astype(np.uint8).reshape(n // 512, 16, m))


K, T, S, V, H, C = 512, 2048, 512, 256, 512, 512


def setup_inputs():
    n = np.random.standard_normal
    s = mx_kscale(K)[:, None]
    packed_xT = pack_weight(n((K, T)) * s)
    packed_w1 = pack_fp4(n((K, H)) / np.sqrt(K) / s)
    perm = np.stack([np.random.permutation(S) for _ in range(8)])
    perm2 = np.stack([np.random.permutation(S) for _ in range(8)])
    return {
        "x_words": packed_xT[0],
        "x_scales": packed_xT[1],
        "w1_words": packed_w1[0],
        "w1_scales": packed_w1[1],
        "gs": (np.random.uniform(0.5, 1.5, (K, 1)) / s).astype(np.float32),
        "offs": striped(np.random.permutation(T)[:S]),
        "la": striped8(perm[:, :V]),
        "lb": striped8(perm[:, V:]),
        "ma": striped8(perm2[:, :V]),
        "mb": striped8(perm2[:, V:]),
        "cand": striped(np.random.permutation(T)[:C]),
    }


def reference(x_words, x_scales, w1_words, w1_scales, gs, offs, la, lb, ma, mb, cand):
    x_cand = unpack_weight(x_words, x_scales)[:, unstriped(cand)]
    xq = unpack_weight(x_words, x_scales)[:, unstriped(offs)]
    y = unpack_fp4(w1_words, w1_scales).T @ xq
    x1 = np.maximum(y[np.arange(H)[:, None], runs(la, H)], y[np.arange(H)[:, None], runs(lb, H)])
    n1 = np.minimum(y[np.arange(H)[:, None], runs(la, H)], y[np.arange(H)[:, None], runs(lb, H)])
    h0 = np.zeros((H, S))
    h0[np.arange(H)[:, None], runs(la, H)] = n1
    h = h0.copy()
    h[np.arange(H)[:, None], runs(lb, H)] = x1
    x2 = np.maximum(h[np.arange(H)[:, None], runs(ma, H)], h[np.arange(H)[:, None], runs(mb, H)])
    n2 = np.minimum(h[np.arange(H)[:, None], runs(ma, H)], h[np.arange(H)[:, None], runs(mb, H)])
    h2 = np.zeros((H, S))
    h2[np.arange(H)[:, None], runs(ma, H)] = n2
    h3 = h2.copy()
    h3[np.arange(H)[:, None], runs(mb, H)] = x2
    z = f64(gs) * h3
    out_0 = 0.0625 * ((x_cand.T @ mxq(z, 0, "e4m3")))
    return (out_0,) + planes(out_0)

@@ -1,0 +1,184 @@
+from contextlib import ExitStack
+
+import concourse.mybir as mybir
+
+K, T, S, V, H, C = 512, 2048, 512, 256, 512, 512
+FLOPS = 2 * K * H * S + 2 * H * C * S
+
+F32 = mybir.dt.float32
+BF16 = mybir.dt.bfloat16
+I32 = mybir.dt.int32
+U32 = mybir.dt.uint32
+U16 = mybir.dt.uint16
+U8 = mybir.dt.uint8
+FP8X4 = mybir.dt.float8_e4m3fn_x4
+FP4X4 = mybir.dt.float4_e2m1fn_x4
+COPY = mybir.ActivationFunctionType.Copy
+ALU = mybir.AluOpType
+
+P = 128
+PACK = 4
+QUADRANTS = 4
+CHUNK = 128
+CHUNKS = S // CHUNK
+PAIR = 2
+OUT_SCALE = 0.0625
+
+
+def load_scale_rows(queue, plane, rows):
+    for q in range(QUADRANTS):
+        queue.dma_start(plane[32 * q : 32 * q + 4, :].bitcast(I32), rows[4 * q : 4 * q + 4, :].bitcast(I32))
+
+
+def tile_picked_bitonic2_none_po_kernel(
+    tc, x_words, x_scales, w1_words, w1_scales, gs, offs, la, lb, ma, mb, cand, out_0, out_1, out_2
+):
+    nc = tc.nc
+    with ExitStack() as ctx:
+        keep = ctx.enter_context(tc.tile_pool(name="keep", bufs=1))
+        psum = ctx.enter_context(tc.psum_pool(name="psum", bufs=1))
+
+        def tile(shape, dtype, name):
+            return keep.tile(shape, dtype, name=name, align_bytes=64)
+
+        x_w = tile([P, T], U32, "x_w")
+        x_s = tile([P, T], U8, "x_s")
+        w_w = tile([P, 2 * H], U8, "w_w")
+        w_s = tile([P, H], U8, "w_s")
+        gs_t = tile([P, PACK], F32, "gs_t")
+        offs_t = tile([P, S // 16], U16, "offs_t")
+        cand_t = tile([P, C // 16], U16, "cand_t")
+        la_t = tile([P, V // 16], U16, "la_t")
+        lb_t = tile([P, V // 16], U16, "lb_t")
+        ma_t = tile([P, V // 16], U16, "ma_t")
+        mb_t = tile([P, V // 16], U16, "mb_t")
+
+        nc.vector.memset(x_s[:].bitcast(I32), 0)
+        nc.vector.memset(w_s[:].bitcast(I32), 0)
+        nc.sync.dma_start(x_w[:].bitcast(I32), x_words[0].rearrange("p c r -> p (c r)").bitcast(I32))
+        load_scale_rows(nc.sync, x_s, x_scales[0])
+        nc.sync.dma_start(offs_t[:], offs)
+        nc.scalar.dma_start(w_w[:].bitcast(I32), w1_words[0].bitcast(I32))
+        load_scale_rows(nc.sync, w_s, w1_scales[0])
+        nc.sync.dma_start(cand_t[:], cand)
+        nc.sync.dma_start(la_t[:], la)
+        nc.sync.dma_start(lb_t[:], lb)
+        nc.sync.dma_start(ma_t[:], ma)
+        nc.sync.dma_start(mb_t[:], mb)
+        nc.sync.dma_start(gs_t[:], gs.rearrange("(p t) o -> p (t o)", t=PACK))
+
+        w_wd = tile([P, PACK, P, 2], U8, "w_wd")
+        w_sd = tile([P, PACK, P], U8, "w_sd")
+        nc.vector.tensor_copy(w_wd[:], w_w[:].rearrange("p (m t b) -> p t m b", t=PACK, b=2))
+        q_w = tile([P, S], U32, "q_w")
+        q_s = tile([P, S], U8, "q_s")
+        nc.vector.tensor_copy(q_s[:], x_s[:].indirect(offs_t[:]))
+        nc.vector.tensor_copy(w_sd[:], w_s[:].rearrange("p (m t) -> p t m", t=PACK))
+        nc.vector.tensor_copy(q_w[:], x_w[:].indirect(offs_t[:]))
+
+        y = []
+        for t in range(PACK):
+            y_ps = psum.tile([P, S], F32, name="y_ps%d" % t)
+            nc.tensor.matmul_mx(
+                out=y_ps[:],
+                lhsT=w_wd[:, t].rearrange("p m b -> p (m b)").bitcast(FP4X4),
+                lhsT_scale=w_sd[:, t, :],
+                rhs=q_w[:].bitcast(FP8X4),
+                rhs_scale=q_s[:],
+                start=True,
+                stop=True,
+            )
+            y.append(tile([P, S], F32, "y%d" % t))
+            nc.scalar.copy(y[t][:], y_ps[:])
+
+        c_w = tile([P, PACK, P], U32, "c_w")
+        c_s = tile([P, C], U8, "c_s")
+        c_sd = tile([P, PACK, P], U8, "c_sd")
+        nc.vector.tensor_copy(c_s[:], x_s[:].indirect(cand_t[:]))
+        nc.vector.tensor_copy(c_w[:].rearrange("p t m -> p m t"), x_w[:].indirect(cand_t[:]))
+
+        h = [tile([P, S], F32, "h%d" % t) for t in range(PACK)]
+        h3 = [tile([P, S], F32, "h3_%d" % t) for t in range(PACK)]
+        stages = [(y, h, la_t, lb_t), (h, h3, ma_t, mb_t)]
+        units = [(stage, first) for stage in range(2) for first in range(0, PACK, PAIR)]
+        at_a = [tile([P, PAIR, V], F32, "at_a%d" % u) for u in range(len(units))]
+        at_b = [tile([P, PAIR, V], F32, "at_b%d" % u) for u in range(len(units))]
+        low = [tile([P, PAIR, V], F32, "low%d" % u) for u in range(len(units))]
+        high = [tile([P, PAIR, V], F32, "high%d" % u) for u in range(len(units))]
+        z_b = [tile([P, CHUNK, PACK], BF16, "z_b%d" % c) for c in range(CHUNKS)]
+
+        def fetch(u):
+            stage, first = units[u]
+            src, dst, list_a, list_b = stages[stage]
+            for i in range(PAIR):
+                nc.vector.tensor_copy(at_a[u][:, i, :], src[first + i][:].indirect(list_a[:]))
+                nc.vector.tensor_copy(at_b[u][:, i, :], src[first + i][:].indirect(list_b[:]))
+
+        def compare(u):
+            nc.vector.tensor_tensor(low[u][:], at_a[u][:], at_b[u][:], ALU.min)
+            nc.vector.tensor_tensor(high[u][:], at_a[u][:], at_b[u][:], ALU.max)
+
+        def put(u):
+            stage, first = units[u]
+            src, dst, list_a, list_b = stages[stage]
+            for i in range(PAIR):
+                nc.vector.tensor_copy(dst[first + i][:].indirect(list_a[:]), low[u][:, i, :])
+            for i in range(PAIR):
+                nc.vector.tensor_copy(dst[first + i][:].indirect(list_b[:]), high[u][:, i, :])
+            if stage == 1:
+                for t in range(first, first + PAIR):
+                    for c in range(CHUNKS):
+                        nc.scalar.activation(
+                            z_b[c][:, :, t], h3[t][:, c * CHUNK : (c + 1) * CHUNK], COPY, scale=gs_t[:, t : t + 1]
+                        )
+
+        fetch(0)
+        nc.vector.tensor_copy(c_sd[:], c_s[:].rearrange("p (m t) -> p t m", t=PACK))
+        for u in range(len(units)):
+            compare(u)
+            if u + 1 < len(units):
+                fetch(u + 1)
+            put(u)
+
+        z_w = tile([P, S], U32, "z_w")
+        z_s = tile([P, S], U8, "z_s")
+        o_w = tile([P, S], U32, "o_w")
+        o_s = tile([P, S], U8, "o_s")
+        out_rows = out_0.rearrange("(p t) j -> p t j", t=PACK)
+        out_words = out_1[0].rearrange("p c r -> p (c r)").bitcast(I32)
+        o_ps = []
+        for c in range(CHUNKS):
+            cols = slice(c * CHUNK, (c + 1) * CHUNK)
+            nc.vector.quantize_mx(
+                out=z_w[:, cols].bitcast(FP8X4), scales=z_s[:, cols], in_=z_b[c][:].rearrange("p j t -> p (j t)")
+            )
+            o_ps.append(psum.tile([P, PACK, CHUNK], F32, name="o_ps%d" % c))
+            for t in range(PACK):
+                nc.tensor.matmul_mx(
+                    out=o_ps[c][:, t, :],
+                    lhsT=c_w[:, t, :].bitcast(FP8X4),
+                    lhsT_scale=c_sd[:, t, :],
+                    rhs=z_w[:, cols].bitcast(FP8X4),
+                    rhs_scale=z_s[:, cols],
+                    start=True,
+                    stop=True,
+                )
+        for c in range(CHUNKS):
+            cols = slice(c * CHUNK, (c + 1) * CHUNK)
+            o_f = tile([P, PACK, CHUNK], F32, "o_f%d" % c)
+            if c == 0:
+                nc.vector.tensor_scalar(o_f[:], o_ps[c][:], OUT_SCALE, None, ALU.mult)
+            else:
+                nc.scalar.mul(o_f[:], o_ps[c][:], OUT_SCALE)
+            nc.sync.dma_start(out_rows[:, :, cols], o_f[:])
+            o_b = tile([P, CHUNK, PACK], BF16, "o_b%d" % c)
+            nc.vector.tensor_copy(o_b[:], o_f[:].rearrange("p t j -> p j t"))
+            nc.vector.quantize_mx(
+                out=o_w[:, cols].bitcast(FP8X4), scales=o_s[:, cols], in_=o_b[:].rearrange("p j t -> p (j t)")
+            )
+            if c % 2 == 1:
+                both = slice((c - 1) * CHUNK, (c + 1) * CHUNK)
+                nc.sync.dma_start(out_words[:, both], o_w[:, both].bitcast(I32))
+        for q in range(QUADRANTS):
+            queue = nc.scalar if q % 2 == 0 else nc.sync
+            queue.dma_start(out_2[0, 4 * q : 4 * q + 4, :].bitcast(I32), o_s[32 * q : 32 * q + 4, :].bitcast(I32))

@@ -25,9 +25,9 @@ PAIR = 2
 OUT_SCALE = 0.0625
 
 
-def load_scale_rows(queue, plane, rows):
+def load_scale_rows(queues, plane, rows):
     for q in range(QUADRANTS):
-        queue.dma_start(plane[32 * q : 32 * q + 4, :].bitcast(I32), rows[4 * q : 4 * q + 4, :].bitcast(I32))
+        queues[q].dma_start(plane[32 * q : 32 * q + 4, :].bitcast(I32), rows[4 * q : 4 * q + 4, :].bitcast(I32))
 
 
 def tile_picked_bitonic2_none_po_kernel(
@@ -54,13 +54,13 @@ def tile_picked_bitonic2_none_po_kernel(
         mb_t = tile([P, V // 16], U16, "mb_t")
 
         nc.vector.memset(x_s[:].bitcast(I32), 0)
-        nc.vector.memset(w_s[:].bitcast(I32), 0)
-        nc.sync.dma_start(x_w[:].bitcast(I32), x_words[0].rearrange("p c r -> p (c r)").bitcast(I32))
-        load_scale_rows(nc.sync, x_s, x_scales[0])
+        nc.gpsimd.memset(w_s[:].bitcast(I32), 0)
         nc.sync.dma_start(offs_t[:], offs)
         nc.scalar.dma_start(w_w[:].bitcast(I32), w1_words[0].bitcast(I32))
-        load_scale_rows(nc.sync, w_s, w1_scales[0])
         nc.sync.dma_start(cand_t[:], cand)
+        nc.sync.dma_start(x_w[:].bitcast(I32), x_words[0].rearrange("p c r -> p (c r)").bitcast(I32))
+        load_scale_rows([nc.scalar] * 4, x_s, x_scales[0])
+        load_scale_rows([nc.scalar, nc.scalar, nc.gpsimd, nc.gpsimd], w_s, w1_scales[0])
         nc.sync.dma_start(la_t[:], la)
         nc.sync.dma_start(lb_t[:], lb)
         nc.sync.dma_start(ma_t[:], ma)
@@ -73,12 +73,12 @@ def tile_picked_bitonic2_none_po_kernel(
         q_w = tile([P, S], U32, "q_w")
         q_s = tile([P, S], U8, "q_s")
         nc.vector.tensor_copy(q_s[:], x_s[:].indirect(offs_t[:]))
-        nc.vector.tensor_copy(w_sd[:], w_s[:].rearrange("p (m t) -> p t m", t=PACK))
         nc.vector.tensor_copy(q_w[:], x_w[:].indirect(offs_t[:]))
+        nc.vector.tensor_copy(w_sd[:], w_s[:].rearrange("p (m t) -> p t m", t=PACK))
 
         y = []
         for t in range(PACK):
-            y_ps = psum.tile([P, S], F32, name="y_ps%d" % t)
+            y_ps = psum.tile([P, S], F32, name="bank%d" % t)
             nc.tensor.matmul_mx(
                 out=y_ps[:],
                 lhsT=w_wd[:, t].rearrange("p m b -> p (m b)").bitcast(FP4X4),
@@ -146,39 +146,62 @@ def tile_picked_bitonic2_none_po_kernel(
         o_s = tile([P, S], U8, "o_s")
         out_rows = out_0.rearrange("(p t) j -> p t j", t=PACK)
         out_words = out_1[0].rearrange("p c r -> p (c r)").bitcast(I32)
-        o_ps = []
-        for c in range(CHUNKS):
-            cols = slice(c * CHUNK, (c + 1) * CHUNK)
+        o_f = [tile([P, PACK, CHUNK], F32, "o_f%d" % c) for c in range(CHUNKS)]
+        o_b = [tile([P, CHUNK, PACK], BF16, "o_b%d" % c) for c in range(CHUNKS)]
+
+        def chunk_cols(c):
+            return slice(c * CHUNK, (c + 1) * CHUNK)
+
+        def score(c):
+            cols = chunk_cols(c)
             nc.vector.quantize_mx(
                 out=z_w[:, cols].bitcast(FP8X4), scales=z_s[:, cols], in_=z_b[c][:].rearrange("p j t -> p (j t)")
             )
-            o_ps.append(psum.tile([P, PACK, CHUNK], F32, name="o_ps%d" % c))
-            for t in range(PACK):
-                nc.tensor.matmul_mx(
-                    out=o_ps[c][:, t, :],
-                    lhsT=c_w[:, t, :].bitcast(FP8X4),
-                    lhsT_scale=c_sd[:, t, :],
-                    rhs=z_w[:, cols].bitcast(FP8X4),
-                    rhs_scale=z_s[:, cols],
-                    start=True,
-                    stop=True,
-                )
-        for c in range(CHUNKS):
-            cols = slice(c * CHUNK, (c + 1) * CHUNK)
-            o_f = tile([P, PACK, CHUNK], F32, "o_f%d" % c)
-            if c == 0:
-                nc.vector.tensor_scalar(o_f[:], o_ps[c][:], OUT_SCALE, None, ALU.mult)
-            else:
-                nc.scalar.mul(o_f[:], o_ps[c][:], OUT_SCALE)
-            nc.sync.dma_start(out_rows[:, :, cols], o_f[:])
-            o_b = tile([P, CHUNK, PACK], BF16, "o_b%d" % c)
-            nc.vector.tensor_copy(o_b[:], o_f[:].rearrange("p t j -> p j t"))
+            banks = []
+            for first in range(0, PACK, PAIR):
+                bank = psum.tile([P, PAIR, CHUNK], F32, name="bank%d" % ((2 * c + first // PAIR + PACK) % 8))
+                for i in range(PAIR):
+                    nc.tensor.matmul_mx(
+                        out=bank[:, i, :],
+                        lhsT=c_w[:, first + i, :].bitcast(FP8X4),
+                        lhsT_scale=c_sd[:, first + i, :],
+                        rhs=z_w[:, cols].bitcast(FP8X4),
+                        rhs_scale=z_s[:, cols],
+                        start=True,
+                        stop=True,
+                    )
+                banks.append(bank)
+            return banks
+
+        def evacuate(c, banks):
+            for half, bank in enumerate(banks):
+                rows = o_f[c][:, PAIR * half : PAIR * (half + 1), :]
+                if c == 0:
+                    nc.vector.tensor_scalar(rows, bank[:], OUT_SCALE, None, ALU.mult)
+                else:
+                    nc.scalar.mul(rows, bank[:], OUT_SCALE)
+            nc.sync.dma_start(out_rows[:, :, chunk_cols(c)], o_f[c][:])
+
+        def regroup(c):
+            nc.vector.tensor_copy(o_b[c][:], o_f[c][:].rearrange("p t j -> p j t"))
+
+        def pack(c):
+            cols = chunk_cols(c)
             nc.vector.quantize_mx(
-                out=o_w[:, cols].bitcast(FP8X4), scales=o_s[:, cols], in_=o_b[:].rearrange("p j t -> p (j t)")
+                out=o_w[:, cols].bitcast(FP8X4), scales=o_s[:, cols], in_=o_b[c][:].rearrange("p j t -> p (j t)")
             )
-            if c % 2 == 1:
-                both = slice((c - 1) * CHUNK, (c + 1) * CHUNK)
-                nc.sync.dma_start(out_words[:, both], o_w[:, both].bitcast(I32))
+
+        scored = [score(c) for c in range(CHUNKS)]
+        for c in range(CHUNKS):
+            evacuate(c, scored[c])
+        for c in range(CHUNKS):
+            regroup(c)
+            if c > 0:
+                pack(c - 1)
+        last = (CHUNKS - 1) * CHUNK
+        nc.sync.dma_start(out_words[:, :last], o_w[:, :last].bitcast(I32))
+        pack(CHUNKS - 1)
+        nc.sync.dma_start(out_words[:, last:], o_w[:, last:].bitcast(I32))
         for q in range(QUADRANTS):
             queue = nc.scalar if q % 2 == 0 else nc.sync
             queue.dma_start(out_2[0, 4 * q : 4 * q + 4, :].bitcast(I32), o_s[32 * q : 32 * q + 4, :].bitcast(I32))

@@ -53,14 +53,14 @@ def tile_picked_bitonic2_none_po_kernel(
         ma_t = tile([P, V // 16], U16, "ma_t")
         mb_t = tile([P, V // 16], U16, "mb_t")
 
+        nc.vector.memset(w_s[:].bitcast(I32), 0)
         nc.vector.memset(x_s[:].bitcast(I32), 0)
-        nc.gpsimd.memset(w_s[:].bitcast(I32), 0)
         nc.sync.dma_start(offs_t[:], offs)
-        nc.scalar.dma_start(w_w[:].bitcast(I32), w1_words[0].bitcast(I32))
+        nc.sync.dma_start(w_w[:].bitcast(I32), w1_words[0].bitcast(I32))
         nc.sync.dma_start(cand_t[:], cand)
+        load_scale_rows([nc.scalar] * 4, w_s, w1_scales[0])
         nc.sync.dma_start(x_w[:].bitcast(I32), x_words[0].rearrange("p c r -> p (c r)").bitcast(I32))
         load_scale_rows([nc.scalar] * 4, x_s, x_scales[0])
-        load_scale_rows([nc.scalar, nc.scalar, nc.gpsimd, nc.gpsimd], w_s, w1_scales[0])
         nc.sync.dma_start(la_t[:], la)
         nc.sync.dma_start(lb_t[:], lb)
         nc.sync.dma_start(ma_t[:], ma)
@@ -72,9 +72,9 @@ def tile_picked_bitonic2_none_po_kernel(
         nc.vector.tensor_copy(w_wd[:], w_w[:].rearrange("p (m t b) -> p t m b", t=PACK, b=2))
         q_w = tile([P, S], U32, "q_w")
         q_s = tile([P, S], U8, "q_s")
-        nc.vector.tensor_copy(q_s[:], x_s[:].indirect(offs_t[:]))
-        nc.vector.tensor_copy(q_w[:], x_w[:].indirect(offs_t[:]))
         nc.vector.tensor_copy(w_sd[:], w_s[:].rearrange("p (m t) -> p t m", t=PACK))
+        nc.vector.tensor_copy(q_w[:], x_w[:].indirect(offs_t[:]))
+        nc.vector.tensor_copy(q_s[:], x_s[:].indirect(offs_t[:]))
 
         y = []
         for t in range(PACK):
@@ -176,10 +176,7 @@ def tile_picked_bitonic2_none_po_kernel(
         def evacuate(c, banks):
             for half, bank in enumerate(banks):
                 rows = o_f[c][:, PAIR * half : PAIR * (half + 1), :]
-                if c == 0:
-                    nc.vector.tensor_scalar(rows, bank[:], OUT_SCALE, None, ALU.mult)
-                else:
-                    nc.scalar.mul(rows, bank[:], OUT_SCALE)
+                nc.scalar.mul(rows, bank[:], OUT_SCALE)
             nc.sync.dma_start(out_rows[:, :, chunk_cols(c)], o_f[c][:])
 
         def regroup(c):
@@ -201,7 +198,7 @@ def tile_picked_bitonic2_none_po_kernel(
         last = (CHUNKS - 1) * CHUNK
         nc.sync.dma_start(out_words[:, :last], o_w[:, :last].bitcast(I32))
         pack(CHUNKS - 1)
-        nc.sync.dma_start(out_words[:, last:], o_w[:, last:].bitcast(I32))
+        nc.scalar.dma_start(out_words[:, last:], o_w[:, last:].bitcast(I32))
         for q in range(QUADRANTS):
-            queue = nc.scalar if q % 2 == 0 else nc.sync
+            queue = nc.sync if q % 2 == 0 else nc.scalar
             queue.dma_start(out_2[0, 4 * q : 4 * q + 4, :].bitcast(I32), o_s[32 * q : 32 * q + 4, :].bitcast(I32))

@@ -53,14 +53,14 @@ def tile_picked_bitonic2_none_po_kernel(
         ma_t = tile([P, V // 16], U16, "ma_t")
         mb_t = tile([P, V // 16], U16, "mb_t")
 
-        nc.vector.memset(w_s[:].bitcast(I32), 0)
         nc.vector.memset(x_s[:].bitcast(I32), 0)
+        nc.gpsimd.memset(w_s[:].bitcast(I32), 0)
         nc.sync.dma_start(offs_t[:], offs)
-        nc.sync.dma_start(w_w[:].bitcast(I32), w1_words[0].bitcast(I32))
+        nc.scalar.dma_start(w_w[:].bitcast(I32), w1_words[0].bitcast(I32))
         nc.sync.dma_start(cand_t[:], cand)
-        load_scale_rows([nc.scalar] * 4, w_s, w1_scales[0])
         nc.sync.dma_start(x_w[:].bitcast(I32), x_words[0].rearrange("p c r -> p (c r)").bitcast(I32))
         load_scale_rows([nc.scalar] * 4, x_s, x_scales[0])
+        load_scale_rows([nc.scalar] * 3 + [nc.gpsimd], w_s, w1_scales[0])
         nc.sync.dma_start(la_t[:], la)
         nc.sync.dma_start(lb_t[:], lb)
         nc.sync.dma_start(ma_t[:], ma)
@@ -69,15 +69,17 @@ def tile_picked_bitonic2_none_po_kernel(
 
         w_wd = tile([P, PACK, P, 2], U8, "w_wd")
         w_sd = tile([P, PACK, P], U8, "w_sd")
-        nc.vector.tensor_copy(w_wd[:], w_w[:].rearrange("p (m t b) -> p t m b", t=PACK, b=2))
+        nc.gpsimd.tensor_copy(w_wd[:], w_w[:].rearrange("p (m t b) -> p t m b", t=PACK, b=2))
+        nc.gpsimd.tensor_copy(w_sd[:], w_s[:].rearrange("p (m t) -> p t m", t=PACK))
         q_w = tile([P, S], U32, "q_w")
         q_s = tile([P, S], U8, "q_s")
-        nc.vector.tensor_copy(w_sd[:], w_s[:].rearrange("p (m t) -> p t m", t=PACK))
-        nc.vector.tensor_copy(q_w[:], x_w[:].indirect(offs_t[:]))
+        c_s = tile([P, C], U8, "c_s")
         nc.vector.tensor_copy(q_s[:], x_s[:].indirect(offs_t[:]))
+        nc.vector.tensor_copy(c_s[:], x_s[:].indirect(cand_t[:]))
+        nc.vector.tensor_copy(q_w[:], x_w[:].indirect(offs_t[:]))
 
-        y = []
-        for t in range(PACK):
+        y = {}
+        for t in (2, 0, 1, 3):
             y_ps = psum.tile([P, S], F32, name="bank%d" % t)
             nc.tensor.matmul_mx(
                 out=y_ps[:],
@@ -88,19 +90,16 @@ def tile_picked_bitonic2_none_po_kernel(
                 start=True,
                 stop=True,
             )
-            y.append(tile([P, S], F32, "y%d" % t))
+            y[t] = tile([P, S], F32, "y%d" % t)
             nc.scalar.copy(y[t][:], y_ps[:])
 
         c_w = tile([P, PACK, P], U32, "c_w")
-        c_s = tile([P, C], U8, "c_s")
         c_sd = tile([P, PACK, P], U8, "c_sd")
-        nc.vector.tensor_copy(c_s[:], x_s[:].indirect(cand_t[:]))
         nc.vector.tensor_copy(c_w[:].rearrange("p t m -> p m t"), x_w[:].indirect(cand_t[:]))
 
         h = [tile([P, S], F32, "h%d" % t) for t in range(PACK)]
-        h3 = [tile([P, S], F32, "h3_%d" % t) for t in range(PACK)]
-        stages = [(y, h, la_t, lb_t), (h, h3, ma_t, mb_t)]
-        units = [(stage, first) for stage in range(2) for first in range(0, PACK, PAIR)]
+        units = [(stage, planes) for stage in range(2) for planes in ((2, 0), (1, 3))]
+        lists = [(la_t, lb_t), (ma_t, mb_t)]
         at_a = [tile([P, PAIR, V], F32, "at_a%d" % u) for u in range(len(units))]
         at_b = [tile([P, PAIR, V], F32, "at_b%d" % u) for u in range(len(units))]
         low = [tile([P, PAIR, V], F32, "low%d" % u) for u in range(len(units))]
@@ -108,37 +107,53 @@ def tile_picked_bitonic2_none_po_kernel(
         z_b = [tile([P, CHUNK, PACK], BF16, "z_b%d" % c) for c in range(CHUNKS)]
 
         def fetch(u):
-            stage, first = units[u]
-            src, dst, list_a, list_b = stages[stage]
-            for i in range(PAIR):
-                nc.vector.tensor_copy(at_a[u][:, i, :], src[first + i][:].indirect(list_a[:]))
-                nc.vector.tensor_copy(at_b[u][:, i, :], src[first + i][:].indirect(list_b[:]))
+            stage, planes = units[u]
+            list_a, list_b = lists[stage]
+            src = y if stage == 0 else h
+            for i, t in enumerate(planes):
+                nc.vector.tensor_copy(at_a[u][:, i, :], src[t][:].indirect(list_a[:]))
+                nc.vector.tensor_copy(at_b[u][:, i, :], src[t][:].indirect(list_b[:]))
 
         def compare(u):
             nc.vector.tensor_tensor(low[u][:], at_a[u][:], at_b[u][:], ALU.min)
             nc.vector.tensor_tensor(high[u][:], at_a[u][:], at_b[u][:], ALU.max)
 
-        def put(u):
-            stage, first = units[u]
-            src, dst, list_a, list_b = stages[stage]
-            for i in range(PAIR):
-                nc.vector.tensor_copy(dst[first + i][:].indirect(list_a[:]), low[u][:, i, :])
-            for i in range(PAIR):
-                nc.vector.tensor_copy(dst[first + i][:].indirect(list_b[:]), high[u][:, i, :])
+        h3 = {}
+
+        def weigh(t, c):
+            cols = h3[t][:, c * CHUNK : (c + 1) * CHUNK]
+            if t == PACK - 1:
+                nc.vector.tensor_scalar(z_b[c][:, :, t], cols, gs_t[:, t : t + 1], None, ALU.mult)
+            else:
+                nc.scalar.activation(z_b[c][:, :, t], cols, COPY, scale=gs_t[:, t : t + 1])
+
+        def put_low(u, i):
+            stage, planes = units[u]
+            t = planes[i]
             if stage == 1:
-                for t in range(first, first + PAIR):
-                    for c in range(CHUNKS):
-                        nc.scalar.activation(
-                            z_b[c][:, :, t], h3[t][:, c * CHUNK : (c + 1) * CHUNK], COPY, scale=gs_t[:, t : t + 1]
-                        )
+                h3[t] = tile([P, S], F32, "h3_%d" % min(t, 2))
+            dst = h if stage == 0 else h3
+            nc.vector.tensor_copy(dst[t][:].indirect(lists[stage][0][:]), low[u][:, i, :])
+
+        def put_high(u, i):
+            stage, planes = units[u]
+            t = planes[i]
+            dst = h if stage == 0 else h3
+            nc.vector.tensor_copy(dst[t][:].indirect(lists[stage][1][:]), high[u][:, i, :])
+            if stage == 1 and t < PACK - 1:
+                for c in range(CHUNKS):
+                    weigh(t, c)
 
         fetch(0)
         nc.vector.tensor_copy(c_sd[:], c_s[:].rearrange("p (m t) -> p t m", t=PACK))
         for u in range(len(units)):
             compare(u)
+            put_low(u, 0)
+            put_low(u, 1)
+            put_high(u, 0)
             if u + 1 < len(units):
                 fetch(u + 1)
-            put(u)
+            put_high(u, 1)
 
         z_w = tile([P, S], U32, "z_w")
         z_s = tile([P, S], U8, "z_s")
@@ -188,7 +203,12 @@ def tile_picked_bitonic2_none_po_kernel(
                 out=o_w[:, cols].bitcast(FP8X4), scales=o_s[:, cols], in_=o_b[c][:].rearrange("p j t -> p (j t)")
             )
 
-        scored = [score(c) for c in range(CHUNKS)]
+        weigh(PACK - 1, 0)
+        scored = []
+        for c in range(CHUNKS):
+            if c + 1 < CHUNKS:
+                weigh(PACK - 1, c + 1)
+            scored.append(score(c))
         for c in range(CHUNKS):
             evacuate(c, scored[c])
         for c in range(CHUNKS):

from contextlib import ExitStack

import concourse.mybir as mybir

K, T, S, V, H, C = 512, 2048, 512, 256, 512, 512
FLOPS = 2 * K * H * S + 2 * H * C * S

F32 = mybir.dt.float32
BF16 = mybir.dt.bfloat16
I32 = mybir.dt.int32
U32 = mybir.dt.uint32
U16 = mybir.dt.uint16
U8 = mybir.dt.uint8
FP8X4 = mybir.dt.float8_e4m3fn_x4
FP4X4 = mybir.dt.float4_e2m1fn_x4
COPY = mybir.ActivationFunctionType.Copy
ALU = mybir.AluOpType

P = 128
PACK = 4
QUADRANTS = 4
CHUNK = 128
CHUNKS = S // CHUNK
PAIR = 2
OUT_SCALE = 0.0625


def load_scale_rows(queues, plane, rows):
    for q in range(QUADRANTS):
        queues[q].dma_start(plane[32 * q : 32 * q + 4, :].bitcast(I32), rows[4 * q : 4 * q + 4, :].bitcast(I32))


def tile_picked_bitonic2_none_po_kernel(
    tc, x_words, x_scales, w1_words, w1_scales, gs, offs, la, lb, ma, mb, cand, out_0, out_1, out_2
):
    nc = tc.nc
    with ExitStack() as ctx:
        keep = ctx.enter_context(tc.tile_pool(name="keep", bufs=1))
        psum = ctx.enter_context(tc.psum_pool(name="psum", bufs=1))

        def tile(shape, dtype, name):
            return keep.tile(shape, dtype, name=name, align_bytes=64)

        x_w = tile([P, T], U32, "x_w")
        x_s = tile([P, T], U8, "x_s")
        w_w = tile([P, 2 * H], U8, "w_w")
        w_s = tile([P, H], U8, "w_s")
        gs_t = tile([P, PACK], F32, "gs_t")
        offs_t = tile([P, S // 16], U16, "offs_t")
        cand_t = tile([P, C // 16], U16, "cand_t")
        la_t = tile([P, V // 16], U16, "la_t")
        lb_t = tile([P, V // 16], U16, "lb_t")
        ma_t = tile([P, V // 16], U16, "ma_t")
        mb_t = tile([P, V // 16], U16, "mb_t")

        nc.vector.memset(x_s[:].bitcast(I32), 0)
        nc.gpsimd.memset(w_s[:].bitcast(I32), 0)
        nc.sync.dma_start(offs_t[:], offs)
        nc.scalar.dma_start(w_w[:].bitcast(I32), w1_words[0].bitcast(I32))
        nc.sync.dma_start(cand_t[:], cand)
        nc.sync.dma_start(x_w[:].bitcast(I32), x_words[0].rearrange("p c r -> p (c r)").bitcast(I32))
        load_scale_rows([nc.scalar] * 4, x_s, x_scales[0])
        load_scale_rows([nc.scalar] * 3 + [nc.gpsimd], w_s, w1_scales[0])
        nc.sync.dma_start(la_t[:], la)
        nc.sync.dma_start(lb_t[:], lb)
        nc.sync.dma_start(ma_t[:], ma)
        nc.sync.dma_start(mb_t[:], mb)
        nc.sync.dma_start(gs_t[:], gs.rearrange("(p t) o -> p (t o)", t=PACK))

        w_wd = tile([P, PACK, P, 2], U8, "w_wd")
        w_sd = tile([P, PACK, P], U8, "w_sd")
        nc.gpsimd.tensor_copy(w_wd[:], w_w[:].rearrange("p (m t b) -> p t m b", t=PACK, b=2))
        nc.gpsimd.tensor_copy(w_sd[:], w_s[:].rearrange("p (m t) -> p t m", t=PACK))
        q_w = tile([P, S], U32, "q_w")
        q_s = tile([P, S], U8, "q_s")
        c_s = tile([P, C], U8, "c_s")
        nc.vector.tensor_copy(q_s[:], x_s[:].indirect(offs_t[:]))
        nc.vector.tensor_copy(c_s[:], x_s[:].indirect(cand_t[:]))
        nc.vector.tensor_copy(q_w[:], x_w[:].indirect(offs_t[:]))

        y = {}
        for t in (2, 0, 1, 3):
            y_ps = psum.tile([P, S], F32, name="bank%d" % t)
            nc.tensor.matmul_mx(
                out=y_ps[:],
                lhsT=w_wd[:, t].rearrange("p m b -> p (m b)").bitcast(FP4X4),
                lhsT_scale=w_sd[:, t, :],
                rhs=q_w[:].bitcast(FP8X4),
                rhs_scale=q_s[:],
                start=True,
                stop=True,
            )
            y[t] = tile([P, S], F32, "y%d" % t)
            nc.scalar.copy(y[t][:], y_ps[:])

        c_w = tile([P, PACK, P], U32, "c_w")
        c_sd = tile([P, PACK, P], U8, "c_sd")
        nc.vector.tensor_copy(c_w[:].rearrange("p t m -> p m t"), x_w[:].indirect(cand_t[:]))

        h = [tile([P, S], F32, "h%d" % t) for t in range(PACK)]
        units = [(stage, planes) for stage in range(2) for planes in ((2, 0), (1, 3))]
        lists = [(la_t, lb_t), (ma_t, mb_t)]
        at_a = [tile([P, PAIR, V], F32, "at_a%d" % u) for u in range(len(units))]
        at_b = [tile([P, PAIR, V], F32, "at_b%d" % u) for u in range(len(units))]
        low = [tile([P, PAIR, V], F32, "low%d" % u) for u in range(len(units))]
        high = [tile([P, PAIR, V], F32, "high%d" % u) for u in range(len(units))]
        z_b = [tile([P, CHUNK, PACK], BF16, "z_b%d" % c) for c in range(CHUNKS)]

        def fetch(u):
            stage, planes = units[u]
            list_a, list_b = lists[stage]
            src = y if stage == 0 else h
            for i, t in enumerate(planes):
                nc.vector.tensor_copy(at_a[u][:, i, :], src[t][:].indirect(list_a[:]))
                nc.vector.tensor_copy(at_b[u][:, i, :], src[t][:].indirect(list_b[:]))

        def compare(u):
            nc.vector.tensor_tensor(low[u][:], at_a[u][:], at_b[u][:], ALU.min)
            nc.vector.tensor_tensor(high[u][:], at_a[u][:], at_b[u][:], ALU.max)

        h3 = {}

        def weigh(t, c):
            cols = h3[t][:, c * CHUNK : (c + 1) * CHUNK]
            if t == PACK - 1:
                nc.vector.tensor_scalar(z_b[c][:, :, t], cols, gs_t[:, t : t + 1], None, ALU.mult)
            else:
                nc.scalar.activation(z_b[c][:, :, t], cols, COPY, scale=gs_t[:, t : t + 1])

        def put_low(u, i):
            stage, planes = units[u]
            t = planes[i]
            if stage == 1:
                h3[t] = tile([P, S], F32, "h3_%d" % min(t, 2))
            dst = h if stage == 0 else h3
            nc.vector.tensor_copy(dst[t][:].indirect(lists[stage][0][:]), low[u][:, i, :])

        def put_high(u, i):
            stage, planes = units[u]
            t = planes[i]
            dst = h if stage == 0 else h3
            nc.vector.tensor_copy(dst[t][:].indirect(lists[stage][1][:]), high[u][:, i, :])
            if stage == 1 and t < PACK - 1:
                for c in range(CHUNKS):
                    weigh(t, c)

        fetch(0)
        nc.vector.tensor_copy(c_sd[:], c_s[:].rearrange("p (m t) -> p t m", t=PACK))
        for u in range(len(units)):
            compare(u)
            put_low(u, 0)
            put_low(u, 1)
            put_high(u, 0)
            if u + 1 < len(units):
                fetch(u + 1)
            put_high(u, 1)

        z_w = tile([P, S], U32, "z_w")
        z_s = tile([P, S], U8, "z_s")
        o_w = tile([P, S], U32, "o_w")
        o_s = tile([P, S], U8, "o_s")
        out_rows = out_0.rearrange("(p t) j -> p t j", t=PACK)
        out_words = out_1[0].rearrange("p c r -> p (c r)").bitcast(I32)
        o_f = [tile([P, PACK, CHUNK], F32, "o_f%d" % c) for c in range(CHUNKS)]
        o_b = [tile([P, CHUNK, PACK], BF16, "o_b%d" % c) for c in range(CHUNKS)]

        def chunk_cols(c):
            return slice(c * CHUNK, (c + 1) * CHUNK)

        def score(c):
            cols = chunk_cols(c)
            nc.vector.quantize_mx(
                out=z_w[:, cols].bitcast(FP8X4), scales=z_s[:, cols], in_=z_b[c][:].rearrange("p j t -> p (j t)")
            )
            banks = []
            for first in range(0, PACK, PAIR):
                bank = psum.tile([P, PAIR, CHUNK], F32, name="bank%d" % ((2 * c + first // PAIR + PACK) % 8))
                for i in range(PAIR):
                    nc.tensor.matmul_mx(
                        out=bank[:, i, :],
                        lhsT=c_w[:, first + i, :].bitcast(FP8X4),
                        lhsT_scale=c_sd[:, first + i, :],
                        rhs=z_w[:, cols].bitcast(FP8X4),
                        rhs_scale=z_s[:, cols],
                        start=True,
                        stop=True,
                    )
                banks.append(bank)
            return banks

        def evacuate(c, banks):
            for half, bank in enumerate(banks):
                rows = o_f[c][:, PAIR * half : PAIR * (half + 1), :]
                nc.scalar.mul(rows, bank[:], OUT_SCALE)
            nc.sync.dma_start(out_rows[:, :, chunk_cols(c)], o_f[c][:])

        def regroup(c):
            nc.vector.tensor_copy(o_b[c][:], o_f[c][:].rearrange("p t j -> p j t"))

        def pack(c):
            cols = chunk_cols(c)
            nc.vector.quantize_mx(
                out=o_w[:, cols].bitcast(FP8X4), scales=o_s[:, cols], in_=o_b[c][:].rearrange("p j t -> p (j t)")
            )

        weigh(PACK - 1, 0)
        scored = []
        for c in range(CHUNKS):
            if c + 1 < CHUNKS:
                weigh(PACK - 1, c + 1)
            scored.append(score(c))
        for c in range(CHUNKS):
            evacuate(c, scored[c])
        for c in range(CHUNKS):
            regroup(c)
            if c > 0:
                pack(c - 1)
        last = (CHUNKS - 1) * CHUNK
        nc.sync.dma_start(out_words[:, :last], o_w[:, :last].bitcast(I32))
        pack(CHUNKS - 1)
        nc.scalar.dma_start(out_words[:, last:], o_w[:, last:].bitcast(I32))
        for q in range(QUADRANTS):
            queue = nc.sync if q % 2 == 0 else nc.scalar
            queue.dma_start(out_2[0, 4 * q : 4 * q + 4, :].bitcast(I32), o_s[32 * q : 32 * q + 4, :].bitcast(I32))
